import numpy as np
import ml_dtypes


def mxq(x, axis, fmt="e4m3"):
    dtype, down = {"e4m3": (ml_dtypes.float8_e4m3fn, 7), "e5m2": (ml_dtypes.float8_e5m2, 14)}[fmt]
    v = np.moveaxis(np.asarray(x, np.float32).astype(ml_dtypes.bfloat16).astype(np.float64), axis, -1)
    blocks = v.reshape(v.shape[:-1] + (-1, 32))
    amax = np.abs(blocks).max(-1, keepdims=True)
    byte = np.maximum(np.where(amax > 0, np.frexp(amax)[1] - 1 + 127, 0) - down, 1)
    scale = np.exp2(byte - 127.0)
    codes = (blocks / scale).astype(np.float32).astype(dtype).astype(np.float64)
    return np.moveaxis((codes * scale).reshape(v.shape), -1, axis)


WIDE = False


def mx_kscale(k):
    if not WIDE:
        return np.ones(k)
    levels = np.array([10, -10, 5, -5, 0])
    if k % 512:
        return np.exp2(np.random.permutation(np.resize(levels, k // 32))).repeat(32)
    a = np.empty((k // 512, 16))
    for p in range(k // 512):
        a[p, :8] = np.random.permutation(np.resize(levels, 8))
        for g in range(8):
            far = levels[np.abs(levels - a[p, g]) >= 10]
            a[p, g + 8] = far[np.random.randint(len(far))]
    return np.exp2(a.ravel()).repeat(32)


def f64(x):
    return np.asarray(x).astype(np.float64)


def striped(idx):
    return np.tile(idx.reshape(-1, 16).T, (8, 1)).astype(np.uint16)


def unstriped(offs):
    return offs[:16].T.reshape(-1).astype(np.int64)


E2M1 = np.array([0.0, 0.5, 1.0, 1.5, 2.0, 3.0, 4.0, 6.0, -0.0, -0.5, -1.0, -1.5, -2.0, -3.0, -4.0, -6.0])


def pack_weight(w, fmt):
    k, n = w.shape
    w = f64(np.asarray(w, np.float32).astype(ml_dtypes.bfloat16)).reshape(k // 32, 32, n)
    amax = np.abs(w).max(1)
    if fmt == "e4m3":
        byte = np.frexp(amax)[1] - 1 + 127 - 7
    else:
        mant, ex = np.frexp(amax / 6.0)
        byte = np.where(mant > 0.5, ex, ex - 1) + 127
    byte = np.clip(np.where(amax > 0, byte, 1), 1, 254)
    scaled = (w * np.exp2(127.0 - byte)[:, None, :]).reshape(k, n).astype(np.float32)
    by_word = np.ascontiguousarray(scaled.reshape(k // 512, 128, 4, n).transpose(0, 1, 3, 2))
    if fmt == "e4m3":
        words = by_word.astype(ml_dtypes.float8_e4m3fn).view(np.uint8)
    else:
        c = by_word.astype(ml_dtypes.float4_e2m1fn).view(np.uint8) & 0xF
        words = (c[..., 0::2] | (c[..., 1::2] << 4)).reshape(k // 512, 128, 2 * n)
    return np.ascontiguousarray(words), np.ascontiguousarray(byte.astype(np.uint8).reshape(k // 512, 16, n))


def unpack_weight(words, scales, fmt):
    g, _, n = scales.shape
    words = np.ascontiguousarray(words).reshape(g, 128, n, -1)
    if fmt == "e4m3":
        vals = words.view(ml_dtypes.float8_e4m3fn).astype(np.float64)
    else:
        nib = np.empty((g, 128, n, 4), np.uint8)
        nib[..., 0::2] = words & 0xF
        nib[..., 1::2] = words >> 4
        vals = E2M1[nib]
    vals = vals * np.repeat(np.exp2(scales.astype(np.float64) - 127.0), 8, axis=1)[..., None]
    return vals.transpose(0, 1, 3, 2).reshape(g * 512, n)


def gelu(v):
    return 0.5 * v * (1.0 + np.tanh(np.sqrt(2.0 / np.pi) * (v + 0.044715 * v**3)))


K, H, N, T, S, P = 1024, 1024, 768, 2048, 1024, 512

def setup_inputs():
    n = np.random.standard_normal
    s = mx_kscale(K)[:, None]
    u = mx_kscale(H)[:, None]
    tab_words, tab_scales = pack_weight(n((K, T)) * s, "e4m3")
    w4_words, w4_scales = pack_weight(n((H, N)) / np.sqrt(H) / u, "e2m1")
    return {
        "tab_words": tab_words, "tab_scales": tab_scales,
        "offs": striped(np.random.permutation(T)[:S]),
        "pos1": striped(np.random.permutation(S)[:P]),
        "pos2": striped(np.random.permutation(S)[:P]),
        "w1": (0.9 * n((K, H)) / np.sqrt(K) / s).astype(np.float32),
        "thr": n(H).astype(np.float32),
        "credit": np.random.uniform(1.5, 3.5, H).astype(np.float32),
        "pw": (n((H, P)) * u).astype(np.float32),
        "w4_words": w4_words, "w4_scales": w4_scales,
    }

def reference(tab_words, tab_scales, offs, pos1, pos2, w1, thr, credit, pw, w4_words, w4_scales):
    v = unpack_weight(tab_words, tab_scales, "e4m3")[:, unstriped(offs)]
    w4 = unpack_weight(w4_words, w4_scales, "e2m1")
    h = mxq(f64(w1), 0, "e4m3").T @ v
    a = 1.0 / (1.0 + np.exp(-(h[:, unstriped(pos1)] + f64(thr)[:, None])))
    c = h[:, unstriped(pos2)]
    q = f64(pw) * (f64(credit)[:, None] * a + c)
    y = w4.T @ mxq(q, 0, "e4m3")
    return np.tanh(y)

@@ -1,0 +1,273 @@
+from contextlib import ExitStack
+
+import concourse.mybir as mybir
+
+K, H, N, T, S, M = 1024, 1024, 768, 2048, 1024, 512
+FLOPS = 2 * K * H * S + 2 * H * N * M
+
+F32 = mybir.dt.float32
+BF16 = mybir.dt.bfloat16
+I32 = mybir.dt.int32
+U32 = mybir.dt.uint32
+U16 = mybir.dt.uint16
+U8 = mybir.dt.uint8
+FP8X4 = mybir.dt.float8_e4m3fn_x4
+FP4X4 = mybir.dt.float4_e2m1fn_x4
+ACT = mybir.ActivationFunctionType
+ALU = mybir.AluOpType
+
+P = 128
+PACK = 4
+PASS = P * PACK
+BANK = 512
+HALF = M // 2
+
+
+def tile_list_donor_fallback_fit_kernel(
+    tc, tab_words, tab_scales, offs, pos1, pos2, w1, thr, credit, pw, w4_words, w4_scales, out
+):
+    nc = tc.nc
+    with ExitStack() as ctx:
+        keep = ctx.enter_context(tc.tile_pool(name="keep", bufs=1))
+        psum = ctx.enter_context(tc.psum_pool(name="psum", bufs=1))
+
+        def sb(name, shape, dtype):
+            return keep.tile(shape, dtype, name=name, align_bytes=64)
+
+        def bank(i):
+            return psum.tile([P, BANK], F32, name=f"bank{i}", tag=f"bank{i}")
+
+        offs_sb = sb("offs_sb", [P, S // 16], U16)
+        nc.sync.dma_start(offs_sb[:], offs)
+
+        tab_s = sb("tab_s", [P, T], U8)
+        nc.vector.memset(tab_s[:].bitcast(I32), 0)
+
+        def load_w1(a, b, c0, c1):
+            raw = sb(f"w1raw{a}{b}_{c0}", [P, PACK, c1 - c0], F32)
+            rows = w1[PASS * a : PASS * (a + 1), PASS * b + c0 : PASS * b + c1]
+            nc.sync.dma_start(out=raw[:], in_=rows.rearrange("(p j) c -> p j c", j=PACK))
+            return raw
+
+        def load_tab(a):
+            words = sb(f"tab_w{a}", [P, T], I32)
+            nc.sync.dma_start(out=words[:], in_=tab_words[a].rearrange("p t i -> p (t i)").bitcast(I32))
+            return words
+
+        def load_pw(b):
+            rows = sb(f"pw{b}", [P, PACK, M], F32)
+            nc.sync.dma_start(out=rows[:], in_=pw[PASS * b : PASS * (b + 1), :].rearrange("(p t) m -> p t m", t=PACK))
+            return rows
+
+        raw00 = [load_w1(0, 0, 0, 256)]
+        for Q in range(4):
+            nc.sync.dma_start(
+                out=tab_s[:].bitcast(I32)[32 * Q : 32 * Q + 8, :],
+                in_=tab_scales[:, 4 * Q : 4 * Q + 4, :].bitcast(I32),
+            )
+        raw00.append(load_w1(0, 0, 256, 512))
+        tab_w = [load_tab(0), load_tab(1)]
+        raw10 = [load_w1(1, 0, 0, 256), load_w1(1, 0, 256, 512)]
+        pos1_sb = sb("pos1_sb", [P, M // 16], U16)
+        nc.sync.dma_start(pos1_sb[:], pos1)
+        pos2_sb = sb("pos2_sb", [P, M // 16], U16)
+        nc.sync.dma_start(pos2_sb[:], pos2)
+        thr_sb = sb("thr_sb", [P, 2, PACK], F32)
+        nc.sync.dma_start(out=thr_sb[:], in_=thr.rearrange("(b p t) -> p b t", b=2, t=PACK))
+        credit_sb = sb("credit_sb", [P, 2, PACK], F32)
+        nc.sync.dma_start(out=credit_sb[:], in_=credit.rearrange("(b p t) -> p b t", b=2, t=PACK))
+        raw01 = load_w1(0, 1, 0, 512)
+        raw11 = load_w1(1, 1, 0, 512)
+        pw_sb = [load_pw(0), load_pw(1)]
+        w4_w = sb("w4_w", [P, 2, 2 * N], U8)
+        nc.sync.dma_start(out=w4_w[:].bitcast(I32), in_=w4_words.rearrange("a p c -> p a c").bitcast(I32))
+        w4_s = sb("w4_s", [P, 2, N], U8)
+        nc.vector.memset(w4_s[:].bitcast(I32), 0)
+        for Q in range(4):
+            nc.sync.dma_start(
+                out=w4_s[:].bitcast(I32)[32 * Q : 32 * Q + 4, :, :],
+                in_=w4_scales[:, 4 * Q : 4 * Q + 4, :].rearrange("a r c -> r a c").bitcast(I32),
+            )
+
+        w1_bf = {}
+        w1_c = {}
+        w1_s = {}
+        for a in range(2):
+            for b in range(2):
+                w1_bf[a, b] = sb(f"w1bf{a}{b}", [P, PACK, P, PACK], BF16)
+                w1_c[a, b] = sb(f"w1c{a}{b}", [P, PASS], U32)
+                w1_s[a, b] = sb(f"w1s{a}{b}", [P, PASS], U8)
+
+        def regroup(engine, a, b, raw, m_raw, m0, m1):
+            dst = w1_bf[a, b][:, :, m0:m1, :].rearrange("p t m j -> p m j t")
+            src = raw[:, :, PACK * (m0 - m_raw) : PACK * (m1 - m_raw)].rearrange("p j (m t) -> p m j t", t=PACK)
+            if engine == "vector":
+                nc.vector.tensor_copy(out=dst, in_=src)
+            else:
+                nc.scalar.copy(out=dst, in_=src)
+
+        def quantise_w1(a, b, t0, t1):
+            nc.vector.quantize_mx(
+                out=w1_c[a, b][:, P * t0 : P * t1].bitcast(FP8X4),
+                scales=w1_s[a, b][:, P * t0 : P * t1],
+                in_=w1_bf[a, b][:, t0:t1, :, :].rearrange("p t m j -> p (t m j)"),
+            )
+
+        v_s = sb("v_s", [P, S], U8)
+        v_w = [sb(f"v_w{a}", [P, S], U32) for a in range(2)]
+
+        def gather_words(a, hh):
+            nc.vector.tensor_copy(
+                out=v_w[a][:, BANK * hh : BANK * (hh + 1)],
+                in_=tab_w[a][:].bitcast(U32).indirect(offs_sb[:, 32 * hh : 32 * (hh + 1)]),
+            )
+
+        def stage1_pass(acc, a, b, t, hh):
+            cols = slice(BANK * hh, BANK * (hh + 1))
+            nc.tensor.matmul_mx(
+                out=acc[:],
+                lhsT=w1_c[a, b][:, P * t : P * (t + 1)].bitcast(FP8X4),
+                lhsT_scale=w1_s[a, b][:, P * t : P * (t + 1)],
+                rhs=v_w[a][:, cols].bitcast(FP8X4),
+                rhs_scale=v_s[4 * a : P, cols],
+                start=(a == 0),
+                stop=(a == 1),
+            )
+
+        nc.vector.tensor_copy(out=v_s[:], in_=tab_s[:].indirect(offs_sb[:]))
+        regroup("scalar", 0, 0, raw00[0], 0, 0, 64)
+        regroup("scalar", 0, 0, raw00[1], 64, 64, 128)
+        gather_words(0, 0)
+        quantise_w1(0, 0, 0, 4)
+        gather_words(0, 1)
+        acc0 = {(t, hh): bank(2 * t + hh) for t in range(PACK) for hh in range(2)}
+        for hh in range(2):
+            for t in range(PACK):
+                stage1_pass(acc0[t, hh], 0, 0, t, hh)
+        gather_words(1, 0)
+        gather_words(1, 1)
+        regroup("scalar", 1, 0, raw10[0], 0, 0, 64)
+        regroup("scalar", 1, 0, raw10[1], 64, 64, 84)
+        regroup("vector", 1, 0, raw10[1], 64, 84, 128)
+        for t in range(PACK):
+            quantise_w1(1, 0, t, t + 1)
+            for hh in range(2):
+                stage1_pass(acc0[t, hh], 1, 0, t, hh)
+
+        h_sb = {(b, t): sb(f"h{b}{t}", [P, S], F32) for b in range(2) for t in range(PACK)}
+
+        def evacuate(engine, acc, b, t, hh):
+            dst = h_sb[b, t][:, BANK * hh : BANK * (hh + 1)]
+            if engine == "vector":
+                nc.vector.tensor_copy(out=dst, in_=acc[:])
+            else:
+                nc.scalar.copy(out=dst, in_=acc[:])
+
+        def look(b, t, m0, m1):
+            gate = sb(f"gate{b}{t}_{m0}", [P, m1 - m0], F32)
+            nc.scalar.activation(
+                out=gate[:],
+                in_=h_sb[b, t][:].indirect(pos1_sb[:, m0 // 16 : m1 // 16]),
+                func=ACT.Sigmoid,
+                bias=thr_sb[:, b, t : t + 1],
+            )
+            return gate
+
+        def fallback(b, t, m0, m1):
+            picked = sb(f"picked{b}{t}_{m0}", [P, m1 - m0], F32)
+            nc.vector.tensor_copy(out=picked[:], in_=h_sb[b, t][:].indirect(pos2_sb[:, m0 // 16 : m1 // 16]))
+            return picked
+
+        def combine(total, b, t, gate, picked):
+            nc.vector.scalar_tensor_tensor(
+                out=total[:, t, :],
+                in0=gate[:],
+                scalar=credit_sb[:, b, t : t + 1],
+                in1=picked[:],
+                op0=ALU.mult,
+                op1=ALU.add,
+            )
+
+        def make_q(total, b, m0, m1):
+            q_bf = sb(f"q_bf{b}_{m0}", [P, m1 - m0, PACK], BF16)
+            q_c = sb(f"q_c{b}_{m0}", [P, m1 - m0], U32)
+            q_s = sb(f"q_s{b}_{m0}", [P, m1 - m0], U8)
+            nc.vector.tensor_tensor(
+                out=q_bf[:].rearrange("p (c i) t -> p c t i", i=4),
+                in0=total.rearrange("p t (c i) -> p c t i", i=4),
+                in1=pw_sb[b][:, :, m0:m1].rearrange("p t (c i) -> p c t i", i=4),
+                op=ALU.mult,
+            )
+            nc.vector.quantize_mx(
+                out=q_c[:].bitcast(FP8X4), scales=q_s[:], in_=q_bf[:].rearrange("p m t -> p (m t)")
+            )
+            return q_c, q_s
+
+        total0 = sb("total0", [P, PACK, M], F32)
+        acc1 = {}
+        for t in range(PACK):
+            for hh in range(2):
+                evacuate("vector" if t == 0 else "scalar", acc0[t, hh], 0, t, hh)
+        regroup("vector", 0, 1, raw01, 0, 0, 128)
+        regroup("scalar", 1, 1, raw11, 0, 0, 128)
+        picks = [fallback(0, 0, 0, M)]
+        quantise_w1(0, 1, 0, 4)
+        picks += [fallback(0, t, 0, M) for t in range(1, PACK)]
+        quantise_w1(1, 1, 0, 4)
+        for t in range(PACK):
+            combine(total0, 0, t, look(0, t, 0, M), picks[t])
+        for t in range(PACK):
+            for hh in range(2):
+                acc1[t, hh] = bank(2 * t + hh)
+                for a in range(2):
+                    stage1_pass(acc1[t, hh], a, 1, t, hh)
+        q0_c, q0_s = make_q(total0[:], 0, 0, M)
+
+        def stage2_pass(acc, a, n, slot, q_c, q_s, c0, width, start, stop):
+            nc.tensor.matmul_mx(
+                out=acc[:, width * slot : width * (slot + 1)],
+                lhsT=w4_w[:, a, 2 * P * n : 2 * P * (n + 1)].bitcast(FP4X4),
+                lhsT_scale=w4_s[:, a, P * n : P * (n + 1)],
+                rhs=q_c[:, c0 : c0 + width].bitcast(FP8X4),
+                rhs_scale=q_s[:, c0 : c0 + width],
+                start=start,
+                stop=stop,
+            )
+
+        total1 = [sb(f"total1_{g}", [P, PACK, HALF], F32) for g in range(2)]
+        for t in range(PACK):
+            for hh in range(2):
+                evacuate("scalar", acc1[t, hh], 1, t, hh)
+        picks = {(g, t): fallback(1, t, HALF * g, HALF * (g + 1)) for g in range(2) for t in range(PACK)}
+
+        chunks = [(0, 256, [0, 1, 2]), (256, 128, [3, 4]), (384, 128, [5, 6, 7])]
+        acc2 = {}
+        for m0, width, banks in chunks:
+            per_bank = 6 // len(banks)
+            for i, bk in enumerate(banks):
+                acc2[m0, i] = bank(bk)
+                for slot in range(per_bank):
+                    stage2_pass(acc2[m0, i], 0, per_bank * i + slot, slot, q0_c, q0_s, m0, width, slot == 0, False)
+
+        def finish(m0, width, banks):
+            per_bank = 6 // len(banks)
+            g, c0 = divmod(m0, HALF)
+            q_c, q_s = make_q(total1[g][:, :, c0 : c0 + width], 1, m0, m0 + width)
+            for i in range(len(banks)):
+                for slot in range(per_bank):
+                    stage2_pass(acc2[m0, i], 1, per_bank * i + slot, slot, q_c, q_s, 0, width, False, slot == per_bank - 1)
+                res = sb(f"res{m0}_{i}", [P, per_bank, width], F32)
+                nc.scalar.activation(
+                    out=res[:].rearrange("p s m -> p (s m)"), in_=acc2[m0, i][:, 0 : per_bank * width], func=ACT.Tanh
+                )
+                rows = out[per_bank * P * i : per_bank * P * (i + 1), m0 : m0 + width]
+                nc.sync.dma_start(out=rows.rearrange("(s p) m -> p s m", s=per_bank), in_=res[:])
+
+        gates = {(g, t): look(1, t, HALF * g, HALF * (g + 1)) for g in range(2) for t in range(PACK)}
+        for t in range(PACK):
+            combine(total1[0], 1, t, gates[0, t], picks[0, t])
+        finish(*chunks[0])
+        for t in range(PACK):
+            combine(total1[1], 1, t, gates[1, t], picks[1, t])
+        finish(*chunks[1])
+        finish(*chunks[2])

@@ -43,8 +43,13 @@ def tile_list_donor_fallback_fit_kernel(
         tab_s = sb("tab_s", [P, T], U8)
         nc.vector.memset(tab_s[:].bitcast(I32), 0)
 
+        warm = sb("warm", [P, 2], F32)
+        nc.gpsimd.memset(warm[:, 0:1], 0.0)
+        nc.scalar.activation(out=warm[:, 1:2], in_=warm[:, 0:1], func=ACT.Sigmoid)
+
         def load_w1(a, b, c0, c1):
-            raw = sb(f"w1raw{a}{b}_{c0}", [P, PACK, c1 - c0], F32)
+            name = f"w1raw{a}{b}_{c0}"
+            raw = keep.tile([P, PACK, c1 - c0], F32, name=name, tag=name, align_bytes=64)
             rows = w1[PASS * a : PASS * (a + 1), PASS * b + c0 : PASS * b + c1]
             nc.sync.dma_start(out=raw[:], in_=rows.rearrange("(p j) c -> p j c", j=PACK))
             return raw
@@ -147,8 +152,7 @@ def tile_list_donor_fallback_fit_kernel(
         gather_words(1, 0)
         gather_words(1, 1)
         regroup("scalar", 1, 0, raw10[0], 0, 0, 64)
-        regroup("scalar", 1, 0, raw10[1], 64, 64, 84)
-        regroup("vector", 1, 0, raw10[1], 64, 84, 128)
+        regroup("vector", 1, 0, raw10[1], 64, 64, 128)
         for t in range(PACK):
             quantise_w1(1, 0, t, t + 1)
             for hh in range(2):
@@ -164,7 +168,7 @@ def tile_list_donor_fallback_fit_kernel(
                 nc.scalar.copy(out=dst, in_=acc[:])
 
         def look(b, t, m0, m1):
-            gate = sb(f"gate{b}{t}_{m0}", [P, m1 - m0], F32)
+            gate = keep.tile([P, m1 - m0], F32, name=f"gate{b}{t}_{m0}", tag=f"gate{b}", bufs=(4, 2)[b], align_bytes=64)
             nc.scalar.activation(
                 out=gate[:],
                 in_=h_sb[b, t][:].indirect(pos1_sb[:, m0 // 16 : m1 // 16]),
@@ -173,19 +177,20 @@ def tile_list_donor_fallback_fit_kernel(
             )
             return gate
 
-        def fallback(b, t, m0, m1):
-            picked = sb(f"picked{b}{t}_{m0}", [P, m1 - m0], F32)
-            nc.vector.tensor_copy(out=picked[:], in_=h_sb[b, t][:].indirect(pos2_sb[:, m0 // 16 : m1 // 16]))
-            return picked
+        def credited(engine, scaled, b, t, gate):
+            if engine == "vector":
+                nc.vector.tensor_scalar(
+                    out=scaled, in0=gate[:], scalar1=credit_sb[:, b, t : t + 1], scalar2=None, op0=ALU.mult
+                )
+            else:
+                nc.scalar.activation(out=scaled, in_=gate[:], func=ACT.Copy, scale=credit_sb[:, b, t : t + 1])
 
-        def combine(total, b, t, gate, picked):
-            nc.vector.scalar_tensor_tensor(
+        def add_fallback(total, b, t, scaled, m0, m1):
+            nc.vector.tensor_tensor(
                 out=total[:, t, :],
-                in0=gate[:],
-                scalar=credit_sb[:, b, t : t + 1],
-                in1=picked[:],
-                op0=ALU.mult,
-                op1=ALU.add,
+                in0=h_sb[b, t][:].indirect(pos2_sb[:, m0 // 16 : m1 // 16]),
+                in1=scaled,
+                op=ALU.add,
             )
 
         def make_q(total, b, m0, m1):
@@ -205,17 +210,19 @@ def tile_list_donor_fallback_fit_kernel(
 
         total0 = sb("total0", [P, PACK, M], F32)
         acc1 = {}
-        for t in range(PACK):
-            for hh in range(2):
-                evacuate("vector" if t == 0 else "scalar", acc0[t, hh], 0, t, hh)
+        for hh in range(2):
+            evacuate("vector", acc0[0, hh], 0, 0, hh)
         regroup("vector", 0, 1, raw01, 0, 0, 128)
-        regroup("scalar", 1, 1, raw11, 0, 0, 128)
-        picks = [fallback(0, 0, 0, M)]
         quantise_w1(0, 1, 0, 4)
-        picks += [fallback(0, t, 0, M) for t in range(1, PACK)]
+        regroup("vector", 1, 1, raw11, 0, 0, 128)
         quantise_w1(1, 1, 0, 4)
+        scaled0 = keep.tile([P, PACK, M], F32, name="scaled0", tag="w1raw11_0", align_bytes=64)
         for t in range(PACK):
-            combine(total0, 0, t, look(0, t, 0, M), picks[t])
+            if t + 1 < PACK:
+                for hh in range(2):
+                    evacuate("scalar", acc0[t + 1, hh], 0, t + 1, hh)
+            credited("vector", scaled0[:, t, :], 0, t, look(0, t, 0, M))
+            add_fallback(total0, 0, t, scaled0[:, t, :], 0, M)
         for t in range(PACK):
             for hh in range(2):
                 acc1[t, hh] = bank(2 * t + hh)
@@ -234,15 +241,18 @@ def tile_list_donor_fallback_fit_kernel(
                 stop=stop,
             )
 
+        scaled1 = [sb(f"scaled1_{g}", [P, PACK, HALF], F32) for g in range(2)]
         total1 = [sb(f"total1_{g}", [P, PACK, HALF], F32) for g in range(2)]
         for t in range(PACK):
             for hh in range(2):
                 evacuate("scalar", acc1[t, hh], 1, t, hh)
-        picks = {(g, t): fallback(1, t, HALF * g, HALF * (g + 1)) for g in range(2) for t in range(PACK)}
+            credited("scalar", scaled1[0][:, t, :], 1, t, look(1, t, 0, HALF))
+            add_fallback(total1[0], 1, t, scaled1[0][:, t, :], 0, HALF)
 
-        chunks = [(0, 256, [0, 1, 2]), (256, 128, [3, 4]), (384, 128, [5, 6, 7])]
+        chunks = [(0, 256, [0, 1, 2]), (256, 128, [0, 1]), (384, 128, [3, 4, 2])]
         acc2 = {}
-        for m0, width, banks in chunks:
+
+        def begin(m0, width, banks):
             per_bank = 6 // len(banks)
             for i, bk in enumerate(banks):
                 acc2[m0, i] = bank(bk)
@@ -263,11 +273,13 @@ def tile_list_donor_fallback_fit_kernel(
                 rows = out[per_bank * P * i : per_bank * P * (i + 1), m0 : m0 + width]
                 nc.sync.dma_start(out=rows.rearrange("(s p) m -> p s m", s=per_bank), in_=res[:])
 
-        gates = {(g, t): look(1, t, HALF * g, HALF * (g + 1)) for g in range(2) for t in range(PACK)}
         for t in range(PACK):
-            combine(total1[0], 1, t, gates[0, t], picks[0, t])
+            credited("scalar", scaled1[1][:, t, :], 1, t, look(1, t, HALF, M))
+        begin(*chunks[0])
         finish(*chunks[0])
+        begin(*chunks[1])
+        begin(*chunks[2])
         for t in range(PACK):
-            combine(total1[1], 1, t, gates[1, t], picks[1, t])
+            add_fallback(total1[1], 1, t, scaled1[1][:, t, :], HALF, M)
         finish(*chunks[1])
         finish(*chunks[2])

@@ -20,7 +20,16 @@ P = 128
 PACK = 4
 PASS = P * PACK
 BANK = 512
+PER_COLUMN = 16
+QUADRANT = 32
+SCALE_ROWS = 4
+LINE = 4
 HALF = M // 2
+N_TILES = N // P
+
+CHUNKS = [(0, 256, [0, 1, 2]), (256, 128, [0, 1]), (384, 128, [3, 4, 2])]
+
+VECTOR_GATES = 2
 
 
 def tile_list_donor_fallback_fit_kernel(
@@ -31,13 +40,19 @@ def tile_list_donor_fallback_fit_kernel(
         keep = ctx.enter_context(tc.tile_pool(name="keep", bufs=1))
         psum = ctx.enter_context(tc.psum_pool(name="psum", bufs=1))
 
-        def sb(name, shape, dtype):
-            return keep.tile(shape, dtype, name=name, align_bytes=64)
+        def sb(name, shape, dtype, tag=None, bufs=1):
+            return keep.tile(shape, dtype, name=name, tag=tag or name, bufs=bufs, align_bytes=64)
 
         def bank(i):
             return psum.tile([P, BANK], F32, name=f"bank{i}", tag=f"bank{i}")
 
-        offs_sb = sb("offs_sb", [P, S // 16], U16)
+        def copy(engine, dst, src):
+            if engine == "vector":
+                nc.vector.tensor_copy(out=dst, in_=src)
+            else:
+                nc.scalar.copy(out=dst, in_=src)
+
+        offs_sb = sb("offs_sb", [P, S // PER_COLUMN], U16)
         nc.sync.dma_start(offs_sb[:], offs)
 
         tab_s = sb("tab_s", [P, T], U8)
@@ -48,8 +63,7 @@ def tile_list_donor_fallback_fit_kernel(
         nc.scalar.activation(out=warm[:, 1:2], in_=warm[:, 0:1], func=ACT.Sigmoid)
 
         def load_w1(a, b, c0, c1):
-            name = f"w1raw{a}{b}_{c0}"
-            raw = keep.tile([P, PACK, c1 - c0], F32, name=name, tag=name, align_bytes=64)
+            raw = sb(f"w1raw{a}{b}_{c0}", [P, PACK, c1 - c0], F32)
             rows = w1[PASS * a : PASS * (a + 1), PASS * b + c0 : PASS * b + c1]
             nc.sync.dma_start(out=raw[:], in_=rows.rearrange("(p j) c -> p j c", j=PACK))
             return raw
@@ -59,39 +73,42 @@ def tile_list_donor_fallback_fit_kernel(
             nc.sync.dma_start(out=words[:], in_=tab_words[a].rearrange("p t i -> p (t i)").bitcast(I32))
             return words
 
+        def load_by_channel(name, vec):
+            cols = sb(name, [P, 2, PACK], F32)
+            nc.sync.dma_start(out=cols[:], in_=vec.rearrange("(b p t) -> p b t", b=2, t=PACK))
+            return cols
+
         def load_pw(b):
             rows = sb(f"pw{b}", [P, PACK, M], F32)
             nc.sync.dma_start(out=rows[:], in_=pw[PASS * b : PASS * (b + 1), :].rearrange("(p t) m -> p t m", t=PACK))
             return rows
 
-        raw00 = [load_w1(0, 0, 0, 256)]
-        for Q in range(4):
+        raw00 = [load_w1(0, 0, 0, PASS // 2)]
+        for Q in range(P // QUADRANT):
             nc.sync.dma_start(
-                out=tab_s[:].bitcast(I32)[32 * Q : 32 * Q + 8, :],
-                in_=tab_scales[:, 4 * Q : 4 * Q + 4, :].bitcast(I32),
+                out=tab_s[:].bitcast(I32)[QUADRANT * Q : QUADRANT * Q + 2 * SCALE_ROWS, :],
+                in_=tab_scales[:, SCALE_ROWS * Q : SCALE_ROWS * (Q + 1), :].bitcast(I32),
             )
-        raw00.append(load_w1(0, 0, 256, 512))
+        raw00.append(load_w1(0, 0, PASS // 2, PASS))
         tab_w = [load_tab(0), load_tab(1)]
-        raw10 = [load_w1(1, 0, 0, 256), load_w1(1, 0, 256, 512)]
-        pos1_sb = sb("pos1_sb", [P, M // 16], U16)
+        raw10 = [load_w1(1, 0, 0, PASS // 2), load_w1(1, 0, PASS // 2, PASS)]
+        pos1_sb = sb("pos1_sb", [P, M // PER_COLUMN], U16)
         nc.sync.dma_start(pos1_sb[:], pos1)
-        pos2_sb = sb("pos2_sb", [P, M // 16], U16)
+        thr_sb = load_by_channel("thr_sb", thr)
+        raw01 = load_w1(0, 1, 0, PASS)
+        credit_sb = load_by_channel("credit_sb", credit)
+        pos2_sb = sb("pos2_sb", [P, M // PER_COLUMN], U16)
         nc.sync.dma_start(pos2_sb[:], pos2)
-        thr_sb = sb("thr_sb", [P, 2, PACK], F32)
-        nc.sync.dma_start(out=thr_sb[:], in_=thr.rearrange("(b p t) -> p b t", b=2, t=PACK))
-        credit_sb = sb("credit_sb", [P, 2, PACK], F32)
-        nc.sync.dma_start(out=credit_sb[:], in_=credit.rearrange("(b p t) -> p b t", b=2, t=PACK))
-        raw01 = load_w1(0, 1, 0, 512)
-        raw11 = load_w1(1, 1, 0, 512)
+        raw11 = load_w1(1, 1, 0, PASS)
         pw_sb = [load_pw(0), load_pw(1)]
         w4_w = sb("w4_w", [P, 2, 2 * N], U8)
         nc.sync.dma_start(out=w4_w[:].bitcast(I32), in_=w4_words.rearrange("a p c -> p a c").bitcast(I32))
         w4_s = sb("w4_s", [P, 2, N], U8)
         nc.vector.memset(w4_s[:].bitcast(I32), 0)
-        for Q in range(4):
+        for Q in range(P // QUADRANT):
             nc.sync.dma_start(
-                out=w4_s[:].bitcast(I32)[32 * Q : 32 * Q + 4, :, :],
-                in_=w4_scales[:, 4 * Q : 4 * Q + 4, :].rearrange("a r c -> r a c").bitcast(I32),
+                out=w4_s[:].bitcast(I32)[QUADRANT * Q : QUADRANT * Q + SCALE_ROWS, :, :],
+                in_=w4_scales[:, SCALE_ROWS * Q : SCALE_ROWS * (Q + 1), :].rearrange("a r c -> r a c").bitcast(I32),
             )
 
         w1_bf = {}
@@ -103,92 +120,88 @@ def tile_list_donor_fallback_fit_kernel(
                 w1_c[a, b] = sb(f"w1c{a}{b}", [P, PASS], U32)
                 w1_s[a, b] = sb(f"w1s{a}{b}", [P, PASS], U8)
 
-        def regroup(engine, a, b, raw, m_raw, m0, m1):
-            dst = w1_bf[a, b][:, :, m0:m1, :].rearrange("p t m j -> p m j t")
-            src = raw[:, :, PACK * (m0 - m_raw) : PACK * (m1 - m_raw)].rearrange("p j (m t) -> p m j t", t=PACK)
-            if engine == "vector":
-                nc.vector.tensor_copy(out=dst, in_=src)
-            else:
-                nc.scalar.copy(out=dst, in_=src)
+        def regroup(engine, a, b, raw, c0, c1):
+            dst = w1_bf[a, b][:, :, c0:c1, :].rearrange("p t c j -> p c j t")
+            copy(engine, dst, raw[:].rearrange("p j (c t) -> p c j t", t=PACK))
 
         def quantise_w1(a, b, t0, t1):
             nc.vector.quantize_mx(
                 out=w1_c[a, b][:, P * t0 : P * t1].bitcast(FP8X4),
                 scales=w1_s[a, b][:, P * t0 : P * t1],
-                in_=w1_bf[a, b][:, t0:t1, :, :].rearrange("p t m j -> p (t m j)"),
+                in_=w1_bf[a, b][:, t0:t1, :, :].rearrange("p t c j -> p (t c j)"),
             )
 
         v_s = sb("v_s", [P, S], U8)
         v_w = [sb(f"v_w{a}", [P, S], U32) for a in range(2)]
 
-        def gather_words(a, hh):
+        def gather_words(a, u):
+            entries = offs_sb[:, BANK // PER_COLUMN * u : BANK // PER_COLUMN * (u + 1)]
             nc.vector.tensor_copy(
-                out=v_w[a][:, BANK * hh : BANK * (hh + 1)],
-                in_=tab_w[a][:].bitcast(U32).indirect(offs_sb[:, 32 * hh : 32 * (hh + 1)]),
+                out=v_w[a][:, BANK * u : BANK * (u + 1)], in_=tab_w[a][:].bitcast(U32).indirect(entries)
             )
 
-        def stage1_pass(acc, a, b, t, hh):
-            cols = slice(BANK * hh, BANK * (hh + 1))
+        def stage1_pass(acc, a, b, t, u):
+            cols = slice(BANK * u, BANK * (u + 1))
             nc.tensor.matmul_mx(
                 out=acc[:],
                 lhsT=w1_c[a, b][:, P * t : P * (t + 1)].bitcast(FP8X4),
                 lhsT_scale=w1_s[a, b][:, P * t : P * (t + 1)],
                 rhs=v_w[a][:, cols].bitcast(FP8X4),
-                rhs_scale=v_s[4 * a : P, cols],
+                rhs_scale=v_s[SCALE_ROWS * a : P, cols],
                 start=(a == 0),
                 stop=(a == 1),
             )
 
         nc.vector.tensor_copy(out=v_s[:], in_=tab_s[:].indirect(offs_sb[:]))
-        regroup("scalar", 0, 0, raw00[0], 0, 0, 64)
-        regroup("scalar", 0, 0, raw00[1], 64, 64, 128)
+        regroup("scalar", 0, 0, raw00[0], 0, P // 2)
+        regroup("scalar", 0, 0, raw00[1], P // 2, P)
         gather_words(0, 0)
-        quantise_w1(0, 0, 0, 4)
+        quantise_w1(0, 0, 0, PACK)
         gather_words(0, 1)
-        acc0 = {(t, hh): bank(2 * t + hh) for t in range(PACK) for hh in range(2)}
-        for hh in range(2):
+        acc0 = {(t, u): bank(2 * t + u) for t in range(PACK) for u in range(2)}
+        for u in range(2):
             for t in range(PACK):
-                stage1_pass(acc0[t, hh], 0, 0, t, hh)
+                stage1_pass(acc0[t, u], 0, 0, t, u)
         gather_words(1, 0)
         gather_words(1, 1)
-        regroup("scalar", 1, 0, raw10[0], 0, 0, 64)
-        regroup("vector", 1, 0, raw10[1], 64, 64, 128)
+        regroup("scalar", 1, 0, raw10[0], 0, P // 2)
+        regroup("vector", 1, 0, raw10[1], P // 2, P)
         for t in range(PACK):
             quantise_w1(1, 0, t, t + 1)
-            for hh in range(2):
-                stage1_pass(acc0[t, hh], 1, 0, t, hh)
+            for u in range(2):
+                stage1_pass(acc0[t, u], 1, 0, t, u)
 
         h_sb = {(b, t): sb(f"h{b}{t}", [P, S], F32) for b in range(2) for t in range(PACK)}
 
-        def evacuate(engine, acc, b, t, hh):
-            dst = h_sb[b, t][:, BANK * hh : BANK * (hh + 1)]
-            if engine == "vector":
-                nc.vector.tensor_copy(out=dst, in_=acc[:])
-            else:
-                nc.scalar.copy(out=dst, in_=acc[:])
+        def evacuate(engine, acc, b, t):
+            for u in range(2):
+                copy(engine, h_sb[b, t][:, BANK * u : BANK * (u + 1)], acc[t, u][:])
 
-        def look(b, t, m0, m1):
-            gate = keep.tile([P, m1 - m0], F32, name=f"gate{b}{t}_{m0}", tag=f"gate{b}", bufs=(4, 2)[b], align_bytes=64)
+        def look(b, t, m0, m1, in_ring):
+            name = f"gate{b}{t}_{m0}"
+            if in_ring:
+                gate = sb(name, [P, m1 - m0], F32, tag="gate_ring", bufs=2)
+            else:
+                gate = sb(name, [P, m1 - m0], F32)
             nc.scalar.activation(
                 out=gate[:],
-                in_=h_sb[b, t][:].indirect(pos1_sb[:, m0 // 16 : m1 // 16]),
+                in_=h_sb[b, t][:].indirect(pos1_sb[:, m0 // PER_COLUMN : m1 // PER_COLUMN]),
                 func=ACT.Sigmoid,
                 bias=thr_sb[:, b, t : t + 1],
             )
             return gate
 
-        def credited(engine, scaled, b, t, gate):
+        def scale_gate(engine, scaled, b, t, gate):
+            factor = credit_sb[:, b, t : t + 1]
             if engine == "vector":
-                nc.vector.tensor_scalar(
-                    out=scaled, in0=gate[:], scalar1=credit_sb[:, b, t : t + 1], scalar2=None, op0=ALU.mult
-                )
+                nc.vector.tensor_scalar(out=scaled, in0=gate[:], scalar1=factor, scalar2=None, op0=ALU.mult)
             else:
-                nc.scalar.activation(out=scaled, in_=gate[:], func=ACT.Copy, scale=credit_sb[:, b, t : t + 1])
+                nc.scalar.activation(out=scaled, in_=gate[:], func=ACT.Copy, scale=factor)
 
         def add_fallback(total, b, t, scaled, m0, m1):
             nc.vector.tensor_tensor(
                 out=total[:, t, :],
-                in0=h_sb[b, t][:].indirect(pos2_sb[:, m0 // 16 : m1 // 16]),
+                in0=h_sb[b, t][:].indirect(pos2_sb[:, m0 // PER_COLUMN : m1 // PER_COLUMN]),
                 in1=scaled,
                 op=ALU.add,
             )
@@ -198,9 +211,9 @@ def tile_list_donor_fallback_fit_kernel(
             q_c = sb(f"q_c{b}_{m0}", [P, m1 - m0], U32)
             q_s = sb(f"q_s{b}_{m0}", [P, m1 - m0], U8)
             nc.vector.tensor_tensor(
-                out=q_bf[:].rearrange("p (c i) t -> p c t i", i=4),
-                in0=total.rearrange("p t (c i) -> p c t i", i=4),
-                in1=pw_sb[b][:, :, m0:m1].rearrange("p t (c i) -> p c t i", i=4),
+                out=q_bf[:].rearrange("p (m i) t -> p m t i", i=LINE),
+                in0=total.rearrange("p t (m i) -> p m t i", i=LINE),
+                in1=pw_sb[b][:, :, m0:m1].rearrange("p t (m i) -> p m t i", i=LINE),
                 op=ALU.mult,
             )
             nc.vector.quantize_mx(
@@ -209,63 +222,65 @@ def tile_list_donor_fallback_fit_kernel(
             return q_c, q_s
 
         total0 = sb("total0", [P, PACK, M], F32)
-        acc1 = {}
-        for hh in range(2):
-            evacuate("vector", acc0[0, hh], 0, 0, hh)
-        regroup("vector", 0, 1, raw01, 0, 0, 128)
-        quantise_w1(0, 1, 0, 4)
-        regroup("vector", 1, 1, raw11, 0, 0, 128)
-        quantise_w1(1, 1, 0, 4)
-        scaled0 = keep.tile([P, PACK, M], F32, name="scaled0", tag="w1raw11_0", align_bytes=64)
+        evacuate("vector", acc0, 0, 0)
+        regroup("vector", 0, 1, raw01, 0, P)
+        quantise_w1(0, 1, 0, PACK)
+        regroup("vector", 1, 1, raw11, 0, P)
+        quantise_w1(1, 1, 0, PACK)
+        scaled_tags = ["scaled00", "w1raw11_0", "w1bf11", "w1raw11_0"]
         for t in range(PACK):
             if t + 1 < PACK:
-                for hh in range(2):
-                    evacuate("scalar", acc0[t + 1, hh], 0, t + 1, hh)
-            credited("vector", scaled0[:, t, :], 0, t, look(0, t, 0, M))
-            add_fallback(total0, 0, t, scaled0[:, t, :], 0, M)
+                evacuate("scalar", acc0, 0, t + 1)
+            scaled = sb(f"scaled0{t}", [P, M], F32, tag=scaled_tags[t])
+            scale_gate("vector", scaled[:], 0, t, look(0, t, 0, M, False))
+            add_fallback(total0, 0, t, scaled[:], 0, M)
+        acc1 = {}
         for t in range(PACK):
-            for hh in range(2):
-                acc1[t, hh] = bank(2 * t + hh)
+            for u in range(2):
+                acc1[t, u] = bank(2 * t + u)
                 for a in range(2):
-                    stage1_pass(acc1[t, hh], a, 1, t, hh)
+                    stage1_pass(acc1[t, u], a, 1, t, u)
         q0_c, q0_s = make_q(total0[:], 0, 0, M)
-
-        def stage2_pass(acc, a, n, slot, q_c, q_s, c0, width, start, stop):
-            nc.tensor.matmul_mx(
-                out=acc[:, width * slot : width * (slot + 1)],
-                lhsT=w4_w[:, a, 2 * P * n : 2 * P * (n + 1)].bitcast(FP4X4),
-                lhsT_scale=w4_s[:, a, P * n : P * (n + 1)],
-                rhs=q_c[:, c0 : c0 + width].bitcast(FP8X4),
-                rhs_scale=q_s[:, c0 : c0 + width],
-                start=start,
-                stop=stop,
-            )
 
         scaled1 = [sb(f"scaled1_{g}", [P, PACK, HALF], F32) for g in range(2)]
         total1 = [sb(f"total1_{g}", [P, PACK, HALF], F32) for g in range(2)]
         for t in range(PACK):
-            for hh in range(2):
-                evacuate("scalar", acc1[t, hh], 1, t, hh)
-            credited("scalar", scaled1[0][:, t, :], 1, t, look(1, t, 0, HALF))
+            evacuate("scalar", acc1, 1, t)
+            on_scalar = t >= VECTOR_GATES
+            gate = look(1, t, 0, HALF, on_scalar)
+            scale_gate("scalar" if on_scalar else "vector", scaled1[0][:, t, :], 1, t, gate)
             add_fallback(total1[0], 1, t, scaled1[0][:, t, :], 0, HALF)
 
-        chunks = [(0, 256, [0, 1, 2]), (256, 128, [0, 1]), (384, 128, [3, 4, 2])]
+        def stage2_pass(acc, b, n, slot, q_c, q_s, width, start, stop):
+            nc.tensor.matmul_mx(
+                out=acc[:, width * slot : width * (slot + 1)],
+                lhsT=w4_w[:, b, 2 * P * n : 2 * P * (n + 1)].bitcast(FP4X4),
+                lhsT_scale=w4_s[:, b, P * n : P * (n + 1)],
+                rhs=q_c.bitcast(FP8X4),
+                rhs_scale=q_s,
+                start=start,
+                stop=stop,
+            )
+
         acc2 = {}
 
         def begin(m0, width, banks):
-            per_bank = 6 // len(banks)
-            for i, bk in enumerate(banks):
-                acc2[m0, i] = bank(bk)
+            per_bank = N_TILES // len(banks)
+            cols = slice(m0, m0 + width)
+            for i, index in enumerate(banks):
+                acc2[m0, i] = bank(index)
                 for slot in range(per_bank):
-                    stage2_pass(acc2[m0, i], 0, per_bank * i + slot, slot, q0_c, q0_s, m0, width, slot == 0, False)
+                    n = per_bank * i + slot
+                    stage2_pass(acc2[m0, i], 0, n, slot, q0_c[:, cols], q0_s[:, cols], width, slot == 0, False)
 
         def finish(m0, width, banks):
-            per_bank = 6 // len(banks)
-            g, c0 = divmod(m0, HALF)
-            q_c, q_s = make_q(total1[g][:, :, c0 : c0 + width], 1, m0, m0 + width)
+            per_bank = N_TILES // len(banks)
+            g, first = divmod(m0, HALF)
+            q_c, q_s = make_q(total1[g][:, :, first : first + width], 1, m0, m0 + width)
             for i in range(len(banks)):
                 for slot in range(per_bank):
-                    stage2_pass(acc2[m0, i], 1, per_bank * i + slot, slot, q_c, q_s, 0, width, False, slot == per_bank - 1)
+                    n = per_bank * i + slot
+                    stage2_pass(acc2[m0, i], 1, n, slot, q_c[:], q_s[:], width, False, slot == per_bank - 1)
                 res = sb(f"res{m0}_{i}", [P, per_bank, width], F32)
                 nc.scalar.activation(
                     out=res[:].rearrange("p s m -> p (s m)"), in_=acc2[m0, i][:, 0 : per_bank * width], func=ACT.Tanh
@@ -274,12 +289,12 @@ def tile_list_donor_fallback_fit_kernel(
                 nc.sync.dma_start(out=rows.rearrange("(s p) m -> p s m", s=per_bank), in_=res[:])
 
         for t in range(PACK):
-            credited("scalar", scaled1[1][:, t, :], 1, t, look(1, t, HALF, M))
-        begin(*chunks[0])
-        finish(*chunks[0])
-        begin(*chunks[1])
-        begin(*chunks[2])
+            scale_gate("scalar", scaled1[1][:, t, :], 1, t, look(1, t, HALF, M, True))
+        begin(*CHUNKS[0])
+        finish(*CHUNKS[0])
+        begin(*CHUNKS[1])
+        begin(*CHUNKS[2])
         for t in range(PACK):
             add_fallback(total1[1], 1, t, scaled1[1][:, t, :], HALF, M)
-        finish(*chunks[1])
-        finish(*chunks[2])
+        finish(*CHUNKS[1])
+        finish(*CHUNKS[2])

from contextlib import ExitStack

import concourse.mybir as mybir

K, H, N, T, S, M = 1024, 1024, 768, 2048, 1024, 512
FLOPS = 2 * K * H * S + 2 * H * N * M

F32 = mybir.dt.float32
BF16 = mybir.dt.bfloat16
I32 = mybir.dt.int32
U32 = mybir.dt.uint32
U16 = mybir.dt.uint16
U8 = mybir.dt.uint8
FP8X4 = mybir.dt.float8_e4m3fn_x4
FP4X4 = mybir.dt.float4_e2m1fn_x4
ACT = mybir.ActivationFunctionType
ALU = mybir.AluOpType

P = 128
PACK = 4
PASS = P * PACK
BANK = 512
PER_COLUMN = 16
QUADRANT = 32
SCALE_ROWS = 4
LINE = 4
HALF = M // 2
N_TILES = N // P

CHUNKS = [(0, 256, [0, 1, 2]), (256, 128, [0, 1]), (384, 128, [3, 4, 2])]

VECTOR_GATES = 2


def tile_list_donor_fallback_fit_kernel(
    tc, tab_words, tab_scales, offs, pos1, pos2, w1, thr, credit, pw, w4_words, w4_scales, out
):
    nc = tc.nc
    with ExitStack() as ctx:
        keep = ctx.enter_context(tc.tile_pool(name="keep", bufs=1))
        psum = ctx.enter_context(tc.psum_pool(name="psum", bufs=1))

        def sb(name, shape, dtype, tag=None, bufs=1):
            return keep.tile(shape, dtype, name=name, tag=tag or name, bufs=bufs, align_bytes=64)

        def bank(i):
            return psum.tile([P, BANK], F32, name=f"bank{i}", tag=f"bank{i}")

        def copy(engine, dst, src):
            if engine == "vector":
                nc.vector.tensor_copy(out=dst, in_=src)
            else:
                nc.scalar.copy(out=dst, in_=src)

        offs_sb = sb("offs_sb", [P, S // PER_COLUMN], U16)
        nc.sync.dma_start(offs_sb[:], offs)

        tab_s = sb("tab_s", [P, T], U8)
        nc.vector.memset(tab_s[:].bitcast(I32), 0)

        warm = sb("warm", [P, 2], F32)
        nc.gpsimd.memset(warm[:, 0:1], 0.0)
        nc.scalar.activation(out=warm[:, 1:2], in_=warm[:, 0:1], func=ACT.Sigmoid)

        def load_w1(a, b, c0, c1):
            raw = sb(f"w1raw{a}{b}_{c0}", [P, PACK, c1 - c0], F32)
            rows = w1[PASS * a : PASS * (a + 1), PASS * b + c0 : PASS * b + c1]
            nc.sync.dma_start(out=raw[:], in_=rows.rearrange("(p j) c -> p j c", j=PACK))
            return raw

        def load_tab(a):
            words = sb(f"tab_w{a}", [P, T], I32)
            nc.sync.dma_start(out=words[:], in_=tab_words[a].rearrange("p t i -> p (t i)").bitcast(I32))
            return words

        def load_by_channel(name, vec):
            cols = sb(name, [P, 2, PACK], F32)
            nc.sync.dma_start(out=cols[:], in_=vec.rearrange("(b p t) -> p b t", b=2, t=PACK))
            return cols

        def load_pw(b):
            rows = sb(f"pw{b}", [P, PACK, M], F32)
            nc.sync.dma_start(out=rows[:], in_=pw[PASS * b : PASS * (b + 1), :].rearrange("(p t) m -> p t m", t=PACK))
            return rows

        raw00 = [load_w1(0, 0, 0, PASS // 2)]
        for Q in range(P // QUADRANT):
            nc.sync.dma_start(
                out=tab_s[:].bitcast(I32)[QUADRANT * Q : QUADRANT * Q + 2 * SCALE_ROWS, :],
                in_=tab_scales[:, SCALE_ROWS * Q : SCALE_ROWS * (Q + 1), :].bitcast(I32),
            )
        raw00.append(load_w1(0, 0, PASS // 2, PASS))
        tab_w = [load_tab(0), load_tab(1)]
        raw10 = [load_w1(1, 0, 0, PASS // 2), load_w1(1, 0, PASS // 2, PASS)]
        pos1_sb = sb("pos1_sb", [P, M // PER_COLUMN], U16)
        nc.sync.dma_start(pos1_sb[:], pos1)
        thr_sb = load_by_channel("thr_sb", thr)
        raw01 = load_w1(0, 1, 0, PASS)
        credit_sb = load_by_channel("credit_sb", credit)
        pos2_sb = sb("pos2_sb", [P, M // PER_COLUMN], U16)
        nc.sync.dma_start(pos2_sb[:], pos2)
        raw11 = load_w1(1, 1, 0, PASS)
        pw_sb = [load_pw(0), load_pw(1)]
        w4_w = sb("w4_w", [P, 2, 2 * N], U8)
        nc.sync.dma_start(out=w4_w[:].bitcast(I32), in_=w4_words.rearrange("a p c -> p a c").bitcast(I32))
        w4_s = sb("w4_s", [P, 2, N], U8)
        nc.vector.memset(w4_s[:].bitcast(I32), 0)
        for Q in range(P // QUADRANT):
            nc.sync.dma_start(
                out=w4_s[:].bitcast(I32)[QUADRANT * Q : QUADRANT * Q + SCALE_ROWS, :, :],
                in_=w4_scales[:, SCALE_ROWS * Q : SCALE_ROWS * (Q + 1), :].rearrange("a r c -> r a c").bitcast(I32),
            )

        w1_bf = {}
        w1_c = {}
        w1_s = {}
        for a in range(2):
            for b in range(2):
                w1_bf[a, b] = sb(f"w1bf{a}{b}", [P, PACK, P, PACK], BF16)
                w1_c[a, b] = sb(f"w1c{a}{b}", [P, PASS], U32)
                w1_s[a, b] = sb(f"w1s{a}{b}", [P, PASS], U8)

        def regroup(engine, a, b, raw, c0, c1):
            dst = w1_bf[a, b][:, :, c0:c1, :].rearrange("p t c j -> p c j t")
            copy(engine, dst, raw[:].rearrange("p j (c t) -> p c j t", t=PACK))

        def quantise_w1(a, b, t0, t1):
            nc.vector.quantize_mx(
                out=w1_c[a, b][:, P * t0 : P * t1].bitcast(FP8X4),
                scales=w1_s[a, b][:, P * t0 : P * t1],
                in_=w1_bf[a, b][:, t0:t1, :, :].rearrange("p t c j -> p (t c j)"),
            )

        v_s = sb("v_s", [P, S], U8)
        v_w = [sb(f"v_w{a}", [P, S], U32) for a in range(2)]

        def gather_words(a, u):
            entries = offs_sb[:, BANK // PER_COLUMN * u : BANK // PER_COLUMN * (u + 1)]
            nc.vector.tensor_copy(
                out=v_w[a][:, BANK * u : BANK * (u + 1)], in_=tab_w[a][:].bitcast(U32).indirect(entries)
            )

        def stage1_pass(acc, a, b, t, u):
            cols = slice(BANK * u, BANK * (u + 1))
            nc.tensor.matmul_mx(
                out=acc[:],
                lhsT=w1_c[a, b][:, P * t : P * (t + 1)].bitcast(FP8X4),
                lhsT_scale=w1_s[a, b][:, P * t : P * (t + 1)],
                rhs=v_w[a][:, cols].bitcast(FP8X4),
                rhs_scale=v_s[SCALE_ROWS * a : P, cols],
                start=(a == 0),
                stop=(a == 1),
            )

        nc.vector.tensor_copy(out=v_s[:], in_=tab_s[:].indirect(offs_sb[:]))
        regroup("scalar", 0, 0, raw00[0], 0, P // 2)
        regroup("scalar", 0, 0, raw00[1], P // 2, P)
        gather_words(0, 0)
        quantise_w1(0, 0, 0, PACK)
        gather_words(0, 1)
        acc0 = {(t, u): bank(2 * t + u) for t in range(PACK) for u in range(2)}
        for u in range(2):
            for t in range(PACK):
                stage1_pass(acc0[t, u], 0, 0, t, u)
        gather_words(1, 0)
        gather_words(1, 1)
        regroup("scalar", 1, 0, raw10[0], 0, P // 2)
        regroup("vector", 1, 0, raw10[1], P // 2, P)
        for t in range(PACK):
            quantise_w1(1, 0, t, t + 1)
            for u in range(2):
                stage1_pass(acc0[t, u], 1, 0, t, u)

        h_sb = {(b, t): sb(f"h{b}{t}", [P, S], F32) for b in range(2) for t in range(PACK)}

        def evacuate(engine, acc, b, t):
            for u in range(2):
                copy(engine, h_sb[b, t][:, BANK * u : BANK * (u + 1)], acc[t, u][:])

        def look(b, t, m0, m1, in_ring):
            name = f"gate{b}{t}_{m0}"
            if in_ring:
                gate = sb(name, [P, m1 - m0], F32, tag="gate_ring", bufs=2)
            else:
                gate = sb(name, [P, m1 - m0], F32)
            nc.scalar.activation(
                out=gate[:],
                in_=h_sb[b, t][:].indirect(pos1_sb[:, m0 // PER_COLUMN : m1 // PER_COLUMN]),
                func=ACT.Sigmoid,
                bias=thr_sb[:, b, t : t + 1],
            )
            return gate

        def scale_gate(engine, scaled, b, t, gate):
            factor = credit_sb[:, b, t : t + 1]
            if engine == "vector":
                nc.vector.tensor_scalar(out=scaled, in0=gate[:], scalar1=factor, scalar2=None, op0=ALU.mult)
            else:
                nc.scalar.activation(out=scaled, in_=gate[:], func=ACT.Copy, scale=factor)

        def add_fallback(total, b, t, scaled, m0, m1):
            nc.vector.tensor_tensor(
                out=total[:, t, :],
                in0=h_sb[b, t][:].indirect(pos2_sb[:, m0 // PER_COLUMN : m1 // PER_COLUMN]),
                in1=scaled,
                op=ALU.add,
            )

        def make_q(total, b, m0, m1):
            q_bf = sb(f"q_bf{b}_{m0}", [P, m1 - m0, PACK], BF16)
            q_c = sb(f"q_c{b}_{m0}", [P, m1 - m0], U32)
            q_s = sb(f"q_s{b}_{m0}", [P, m1 - m0], U8)
            nc.vector.tensor_tensor(
                out=q_bf[:].rearrange("p (m i) t -> p m t i", i=LINE),
                in0=total.rearrange("p t (m i) -> p m t i", i=LINE),
                in1=pw_sb[b][:, :, m0:m1].rearrange("p t (m i) -> p m t i", i=LINE),
                op=ALU.mult,
            )
            nc.vector.quantize_mx(
                out=q_c[:].bitcast(FP8X4), scales=q_s[:], in_=q_bf[:].rearrange("p m t -> p (m t)")
            )
            return q_c, q_s

        total0 = sb("total0", [P, PACK, M], F32)
        evacuate("vector", acc0, 0, 0)
        regroup("vector", 0, 1, raw01, 0, P)
        quantise_w1(0, 1, 0, PACK)
        regroup("vector", 1, 1, raw11, 0, P)
        quantise_w1(1, 1, 0, PACK)
        scaled_tags = ["scaled00", "w1raw11_0", "w1bf11", "w1raw11_0"]
        for t in range(PACK):
            if t + 1 < PACK:
                evacuate("scalar", acc0, 0, t + 1)
            scaled = sb(f"scaled0{t}", [P, M], F32, tag=scaled_tags[t])
            scale_gate("vector", scaled[:], 0, t, look(0, t, 0, M, False))
            add_fallback(total0, 0, t, scaled[:], 0, M)
        acc1 = {}
        for t in range(PACK):
            for u in range(2):
                acc1[t, u] = bank(2 * t + u)
                for a in range(2):
                    stage1_pass(acc1[t, u], a, 1, t, u)
        q0_c, q0_s = make_q(total0[:], 0, 0, M)

        scaled1 = [sb(f"scaled1_{g}", [P, PACK, HALF], F32) for g in range(2)]
        total1 = [sb(f"total1_{g}", [P, PACK, HALF], F32) for g in range(2)]
        for t in range(PACK):
            evacuate("scalar", acc1, 1, t)
            on_scalar = t >= VECTOR_GATES
            gate = look(1, t, 0, HALF, on_scalar)
            scale_gate("scalar" if on_scalar else "vector", scaled1[0][:, t, :], 1, t, gate)
            add_fallback(total1[0], 1, t, scaled1[0][:, t, :], 0, HALF)

        def stage2_pass(acc, b, n, slot, q_c, q_s, width, start, stop):
            nc.tensor.matmul_mx(
                out=acc[:, width * slot : width * (slot + 1)],
                lhsT=w4_w[:, b, 2 * P * n : 2 * P * (n + 1)].bitcast(FP4X4),
                lhsT_scale=w4_s[:, b, P * n : P * (n + 1)],
                rhs=q_c.bitcast(FP8X4),
                rhs_scale=q_s,
                start=start,
                stop=stop,
            )

        acc2 = {}

        def begin(m0, width, banks):
            per_bank = N_TILES // len(banks)
            cols = slice(m0, m0 + width)
            for i, index in enumerate(banks):
                acc2[m0, i] = bank(index)
                for slot in range(per_bank):
                    n = per_bank * i + slot
                    stage2_pass(acc2[m0, i], 0, n, slot, q0_c[:, cols], q0_s[:, cols], width, slot == 0, False)

        def finish(m0, width, banks):
            per_bank = N_TILES // len(banks)
            g, first = divmod(m0, HALF)
            q_c, q_s = make_q(total1[g][:, :, first : first + width], 1, m0, m0 + width)
            for i in range(len(banks)):
                for slot in range(per_bank):
                    n = per_bank * i + slot
                    stage2_pass(acc2[m0, i], 1, n, slot, q_c[:], q_s[:], width, False, slot == per_bank - 1)
                res = sb(f"res{m0}_{i}", [P, per_bank, width], F32)
                nc.scalar.activation(
                    out=res[:].rearrange("p s m -> p (s m)"), in_=acc2[m0, i][:, 0 : per_bank * width], func=ACT.Tanh
                )
                rows = out[per_bank * P * i : per_bank * P * (i + 1), m0 : m0 + width]
                nc.sync.dma_start(out=rows.rearrange("(s p) m -> p s m", s=per_bank), in_=res[:])

        for t in range(PACK):
            scale_gate("scalar", scaled1[1][:, t, :], 1, t, look(1, t, HALF, M, True))
        begin(*CHUNKS[0])
        finish(*CHUNKS[0])
        begin(*CHUNKS[1])
        begin(*CHUNKS[2])
        for t in range(PACK):
            add_fallback(total1[1], 1, t, scaled1[1][:, t, :], HALF, M)
        finish(*CHUNKS[1])
        finish(*CHUNKS[2])
